import numpy as np
CORES = [3,11,131,139,259,267,387,395]
N = 8
ROOT = 5
def setup_inputs(rng):
    return {"x": rng.standard_normal((N, 128, N * 2), dtype=np.float32)}
def reference(x):
    return {"y": np.stack([x[ROOT][:, r * 2:(r + 1) * 2] for r in range(N)])}

@@ -1,0 +1,42 @@
+from concourse.bass import DstId, RemoteDMATransfer
+
+SCRATCH = {
+    "xs": ("dram", [128, 16], "float32"),
+}
+SEMAPHORES = ["loaded", "stored", "arrived", "sent"]
+
+OFF_CHIP = 0x00FF
+NENG = 8
+FIRST = (6, 7, 3, 4)
+RELAY = {6: 0, 7: 1, 3: 2}
+
+
+def rank_program(g, core, T, topo):
+    rank = T.rank_of(core)
+    if rank is None:
+        return
+    cores = T.cores
+    if rank == T.root:
+        g.dma_start(T.xs[:, :], T.x[:, :]).then_inc(T.sem.loaded, 16)
+        g.wait_ge(T.sem.loaded, 16)
+        ids = []
+        for r in FIRST:
+            rid, pid = topo.addr(cores[r], core)
+            ids.append(DstId(rid=rid, pnc=pid))
+        g.remote_dma_fused(
+            [RemoteDMATransfer(dst_ids=ids, dma_engine_mask=OFF_CHIP, remote_sem=T.sem.arrived,
+                               srcs=[T.xs[:, :]], dsts=[T.xs[:, :] for r in FIRST], alu_op=0)],
+            local_sem=T.sem.sent)
+        g.dma_start(T.y[:, :], T.x[:, 2 * rank:2 * rank + 2]).then_inc(T.sem.stored, 16)
+        g.wait_ge(T.sem.stored, 16)
+        g.wait_ge(T.sem.sent, NENG)
+        return
+    g.wait_ge(T.sem.arrived, NENG)
+    if rank in RELAY:
+        d = cores[RELAY[rank]]
+        rid, pid = topo.addr(d, core)
+        g.remote_dma(T.xs[:, :], T.xs[:, :], T.sem.arrived, T.sem.sent, pid, rid, OFF_CHIP)
+    g.dma_start(T.y[:, :], T.xs[:, 2 * rank:2 * rank + 2]).then_inc(T.sem.stored, 16)
+    g.wait_ge(T.sem.stored, 16)
+    if rank in RELAY:
+        g.wait_ge(T.sem.sent, NENG)

@@ -2,41 +2,52 @@ from concourse.bass import DstId, RemoteDMATransfer
 
 SCRATCH = {
     "xs": ("dram", [128, 16], "float32"),
+    "far": ("dram", [128, 4], "float32"),
 }
-SEMAPHORES = ["loaded", "stored", "arrived", "sent"]
+SEMAPHORES = ["cut", "loaded", "stored", "passed", "arrived", "sent"]
 
 OFF_CHIP = 0x00FF
-NENG = 8
-FIRST = (6, 7, 3, 4)
-RELAY = {6: 0, 7: 1, 3: 2}
+RELAY = {6: 0, 7: 1}
+DIRECT = (3, 2, 4, 6, 7)
+
+
+def one_to_many(g, T, topo, core, ranks, buf, sem):
+    ids = []
+    for r in ranks:
+        rid, pid = topo.addr(T.cores[r], core)
+        ids.append(DstId(rid=rid, pnc=pid))
+    g.remote_dma_fused(
+        [RemoteDMATransfer(dst_ids=ids, dma_engine_mask=OFF_CHIP, remote_sem=sem,
+                           srcs=[buf[:, :]], dsts=[buf[:, :] for r in ranks], alu_op=0)],
+        local_sem=T.sem.sent)
 
 
 def rank_program(g, core, T, topo):
     rank = T.rank_of(core)
     if rank is None:
         return
-    cores = T.cores
     if rank == T.root:
+        g.dma_start(T.far[:, :], T.x[:, 0:4]).then_inc(T.sem.cut, 16)
         g.dma_start(T.xs[:, :], T.x[:, :]).then_inc(T.sem.loaded, 16)
+        g.wait_ge(T.sem.cut, 16)
+        one_to_many(g, T, topo, core, tuple(RELAY), T.far, T.sem.passed)
         g.wait_ge(T.sem.loaded, 16)
-        ids = []
-        for r in FIRST:
-            rid, pid = topo.addr(cores[r], core)
-            ids.append(DstId(rid=rid, pnc=pid))
-        g.remote_dma_fused(
-            [RemoteDMATransfer(dst_ids=ids, dma_engine_mask=OFF_CHIP, remote_sem=T.sem.arrived,
-                               srcs=[T.xs[:, :]], dsts=[T.xs[:, :] for r in FIRST], alu_op=0)],
-            local_sem=T.sem.sent)
+        one_to_many(g, T, topo, core, DIRECT, T.xs, T.sem.arrived)
         g.dma_start(T.y[:, :], T.x[:, 2 * rank:2 * rank + 2]).then_inc(T.sem.stored, 16)
         g.wait_ge(T.sem.stored, 16)
-        g.wait_ge(T.sem.sent, NENG)
+        g.wait_ge(T.sem.sent, 16)
         return
-    g.wait_ge(T.sem.arrived, NENG)
+    if rank in (0, 1):
+        g.wait_ge(T.sem.passed, 8)
+        g.dma_start(T.y[:, :], T.far[:, 2 * rank:2 * rank + 2]).then_inc(T.sem.stored, 16)
+        g.wait_ge(T.sem.stored, 16)
+        return
     if rank in RELAY:
-        d = cores[RELAY[rank]]
-        rid, pid = topo.addr(d, core)
-        g.remote_dma(T.xs[:, :], T.xs[:, :], T.sem.arrived, T.sem.sent, pid, rid, OFF_CHIP)
+        g.wait_ge(T.sem.passed, 8)
+        rid, pid = topo.addr(T.cores[RELAY[rank]], core)
+        g.remote_dma(T.far[:, :], T.far[:, :], T.sem.passed, T.sem.sent, pid, rid, OFF_CHIP)
+    g.wait_ge(T.sem.arrived, 8)
     g.dma_start(T.y[:, :], T.xs[:, 2 * rank:2 * rank + 2]).then_inc(T.sem.stored, 16)
     g.wait_ge(T.sem.stored, 16)
     if rank in RELAY:
-        g.wait_ge(T.sem.sent, NENG)
+        g.wait_ge(T.sem.sent, 8)

@@ -1,25 +1,22 @@
 from concourse.bass import DstId, RemoteDMATransfer
 
 SCRATCH = {
-    "xs": ("dram", [128, 16], "float32"),
-    "far": ("dram", [128, 4], "float32"),
+    "lo": ("dram", [128, 8], "float32"),
+    "hi": ("dram", [128, 8], "float32"),
 }
-SEMAPHORES = ["cut", "loaded", "stored", "passed", "arrived", "sent"]
+SEMAPHORES = ["cut", "cut2", "stored", "passed", "arrived", "sent"]
 
 OFF_CHIP = 0x00FF
 RELAY = {6: 0, 7: 1}
-DIRECT = (3, 2, 4, 6, 7)
 
 
-def one_to_many(g, T, topo, core, ranks, buf, sem):
+def one_to_many(T, topo, core, ranks, buf, sem, mask):
     ids = []
     for r in ranks:
         rid, pid = topo.addr(T.cores[r], core)
         ids.append(DstId(rid=rid, pnc=pid))
-    g.remote_dma_fused(
-        [RemoteDMATransfer(dst_ids=ids, dma_engine_mask=OFF_CHIP, remote_sem=sem,
-                           srcs=[buf[:, :]], dsts=[buf[:, :] for r in ranks], alu_op=0)],
-        local_sem=T.sem.sent)
+    return RemoteDMATransfer(dst_ids=ids, dma_engine_mask=mask, remote_sem=sem,
+                             srcs=[buf[:, :]], dsts=[buf[:, :] for r in ranks], alu_op=0)
 
 
 def rank_program(g, core, T, topo):
@@ -27,27 +24,29 @@ def rank_program(g, core, T, topo):
     if rank is None:
         return
     if rank == T.root:
-        g.dma_start(T.far[:, :], T.x[:, 0:4]).then_inc(T.sem.cut, 16)
-        g.dma_start(T.xs[:, :], T.x[:, :]).then_inc(T.sem.loaded, 16)
+        g.dma_start(T.lo[:, :], T.x[:, 0:8]).then_inc(T.sem.cut, 16)
+        g.dma_start(T.hi[:, :], T.x[:, 8:16]).then_inc(T.sem.cut2, 16)
         g.wait_ge(T.sem.cut, 16)
-        one_to_many(g, T, topo, core, tuple(RELAY), T.far, T.sem.passed)
-        g.wait_ge(T.sem.loaded, 16)
-        one_to_many(g, T, topo, core, DIRECT, T.xs, T.sem.arrived)
+        g.remote_dma_fused([one_to_many(T, topo, core, tuple(RELAY), T.lo, T.sem.passed, OFF_CHIP)],
+                           local_sem=T.sem.sent)
+        g.wait_ge(T.sem.cut2, 16)
+        g.remote_dma_fused([one_to_many(T, topo, core, (3, 2), T.lo, T.sem.arrived, 0x0F),
+                            one_to_many(T, topo, core, (4, 6, 7), T.hi, T.sem.arrived, 0xF0)],
+                           local_sem=T.sem.sent)
         g.dma_start(T.y[:, :], T.x[:, 2 * rank:2 * rank + 2]).then_inc(T.sem.stored, 16)
         g.wait_ge(T.sem.stored, 16)
         g.wait_ge(T.sem.sent, 16)
         return
-    if rank in (0, 1):
-        g.wait_ge(T.sem.passed, 8)
-        g.dma_start(T.y[:, :], T.far[:, 2 * rank:2 * rank + 2]).then_inc(T.sem.stored, 16)
-        g.wait_ge(T.sem.stored, 16)
-        return
     if rank in RELAY:
         g.wait_ge(T.sem.passed, 8)
         rid, pid = topo.addr(T.cores[RELAY[rank]], core)
-        g.remote_dma(T.far[:, :], T.far[:, :], T.sem.passed, T.sem.sent, pid, rid, OFF_CHIP)
-    g.wait_ge(T.sem.arrived, 8)
-    g.dma_start(T.y[:, :], T.xs[:, 2 * rank:2 * rank + 2]).then_inc(T.sem.stored, 16)
+        g.remote_dma(T.lo[:, :], T.lo[:, :], T.sem.passed, T.sem.sent, pid, rid, OFF_CHIP)
+    if rank in (0, 1):
+        g.wait_ge(T.sem.passed, 8)
+    else:
+        g.wait_ge(T.sem.arrived, 4)
+    src = T.lo[:, 2 * rank:2 * rank + 2] if rank < 4 else T.hi[:, 2 * rank - 8:2 * rank - 6]
+    g.dma_start(T.y[:, :], src).then_inc(T.sem.stored, 16)
     g.wait_ge(T.sem.stored, 16)
     if rank in RELAY:
         g.wait_ge(T.sem.sent, 8)

@@ -7,16 +7,18 @@ SCRATCH = {
 SEMAPHORES = ["cut", "cut2", "stored", "passed", "arrived", "sent"]
 
 OFF_CHIP = 0x00FF
-RELAY = {6: 0, 7: 1}
+RELAY = {6: 0, 7: 1, 3: 2}
 
 
-def one_to_many(T, topo, core, ranks, buf, sem, mask):
+def one_to_many(g, T, topo, core, ranks, buf, sem):
     ids = []
     for r in ranks:
         rid, pid = topo.addr(T.cores[r], core)
         ids.append(DstId(rid=rid, pnc=pid))
-    return RemoteDMATransfer(dst_ids=ids, dma_engine_mask=mask, remote_sem=sem,
-                             srcs=[buf[:, :]], dsts=[buf[:, :] for r in ranks], alu_op=0)
+    g.remote_dma_fused(
+        [RemoteDMATransfer(dst_ids=ids, dma_engine_mask=OFF_CHIP, remote_sem=sem,
+                           srcs=[buf[:, :]], dsts=[buf[:, :] for r in ranks], alu_op=0)],
+        local_sem=T.sem.sent)
 
 
 def rank_program(g, core, T, topo):
@@ -27,24 +29,20 @@ def rank_program(g, core, T, topo):
         g.dma_start(T.lo[:, :], T.x[:, 0:8]).then_inc(T.sem.cut, 16)
         g.dma_start(T.hi[:, :], T.x[:, 8:16]).then_inc(T.sem.cut2, 16)
         g.wait_ge(T.sem.cut, 16)
-        g.remote_dma_fused([one_to_many(T, topo, core, tuple(RELAY), T.lo, T.sem.passed, OFF_CHIP)],
-                           local_sem=T.sem.sent)
+        one_to_many(g, T, topo, core, tuple(RELAY), T.lo, T.sem.passed)
         g.wait_ge(T.sem.cut2, 16)
-        g.remote_dma_fused([one_to_many(T, topo, core, (3, 2), T.lo, T.sem.arrived, 0x0F),
-                            one_to_many(T, topo, core, (4, 6, 7), T.hi, T.sem.arrived, 0xF0)],
-                           local_sem=T.sem.sent)
+        one_to_many(g, T, topo, core, (4, 6, 7), T.hi, T.sem.arrived)
         g.dma_start(T.y[:, :], T.x[:, 2 * rank:2 * rank + 2]).then_inc(T.sem.stored, 16)
         g.wait_ge(T.sem.stored, 16)
         g.wait_ge(T.sem.sent, 16)
         return
-    if rank in RELAY:
+    if rank != 4:
         g.wait_ge(T.sem.passed, 8)
+    if rank in RELAY:
         rid, pid = topo.addr(T.cores[RELAY[rank]], core)
         g.remote_dma(T.lo[:, :], T.lo[:, :], T.sem.passed, T.sem.sent, pid, rid, OFF_CHIP)
-    if rank in (0, 1):
-        g.wait_ge(T.sem.passed, 8)
-    else:
-        g.wait_ge(T.sem.arrived, 4)
+    if rank >= 4:
+        g.wait_ge(T.sem.arrived, 8)
     src = T.lo[:, 2 * rank:2 * rank + 2] if rank < 4 else T.hi[:, 2 * rank - 8:2 * rank - 6]
     g.dma_start(T.y[:, :], src).then_inc(T.sem.stored, 16)
     g.wait_ge(T.sem.stored, 16)

from concourse.bass import DstId, RemoteDMATransfer

SCRATCH = {
    "lo": ("dram", [128, 8], "float32"),
    "hi": ("dram", [128, 8], "float32"),
}
SEMAPHORES = ["cut", "cut2", "stored", "passed", "arrived", "sent"]

OFF_CHIP = 0x00FF
RELAY = {6: 0, 7: 1, 3: 2}


def one_to_many(g, T, topo, core, ranks, buf, sem):
    ids = []
    for r in ranks:
        rid, pid = topo.addr(T.cores[r], core)
        ids.append(DstId(rid=rid, pnc=pid))
    g.remote_dma_fused(
        [RemoteDMATransfer(dst_ids=ids, dma_engine_mask=OFF_CHIP, remote_sem=sem,
                           srcs=[buf[:, :]], dsts=[buf[:, :] for r in ranks], alu_op=0)],
        local_sem=T.sem.sent)


def rank_program(g, core, T, topo):
    rank = T.rank_of(core)
    if rank is None:
        return
    if rank == T.root:
        g.dma_start(T.lo[:, :], T.x[:, 0:8]).then_inc(T.sem.cut, 16)
        g.dma_start(T.hi[:, :], T.x[:, 8:16]).then_inc(T.sem.cut2, 16)
        g.wait_ge(T.sem.cut, 16)
        one_to_many(g, T, topo, core, tuple(RELAY), T.lo, T.sem.passed)
        g.wait_ge(T.sem.cut2, 16)
        one_to_many(g, T, topo, core, (4, 6, 7), T.hi, T.sem.arrived)
        g.dma_start(T.y[:, :], T.x[:, 2 * rank:2 * rank + 2]).then_inc(T.sem.stored, 16)
        g.wait_ge(T.sem.stored, 16)
        g.wait_ge(T.sem.sent, 16)
        return
    if rank != 4:
        g.wait_ge(T.sem.passed, 8)
    if rank in RELAY:
        rid, pid = topo.addr(T.cores[RELAY[rank]], core)
        g.remote_dma(T.lo[:, :], T.lo[:, :], T.sem.passed, T.sem.sent, pid, rid, OFF_CHIP)
    if rank >= 4:
        g.wait_ge(T.sem.arrived, 8)
    src = T.lo[:, 2 * rank:2 * rank + 2] if rank < 4 else T.hi[:, 2 * rank - 8:2 * rank - 6]
    g.dma_start(T.y[:, :], src).then_inc(T.sem.stored, 16)
    g.wait_ge(T.sem.stored, 16)
    if rank in RELAY:
        g.wait_ge(T.sem.sent, 8)
